import numpy as np
import ml_dtypes


def mxq(x, axis, fmt="e4m3"):
    dtype, down = {"e4m3": (ml_dtypes.float8_e4m3fn, 7), "e5m2": (ml_dtypes.float8_e5m2, 14)}[fmt]
    v = np.moveaxis(np.asarray(x, np.float32).astype(ml_dtypes.bfloat16).astype(np.float64), axis, -1)
    blocks = v.reshape(v.shape[:-1] + (-1, 32))
    amax = np.abs(blocks).max(-1, keepdims=True)
    byte = np.maximum(np.where(amax > 0, np.frexp(amax)[1] - 1 + 127, 0) - down, 1)
    scale = np.exp2(byte - 127.0)
    codes = (blocks / scale).astype(np.float32).astype(dtype).astype(np.float64)
    return np.moveaxis((codes * scale).reshape(v.shape), -1, axis)


WIDE = False


def mx_kscale(k):
    if not WIDE:
        return np.ones(k)
    levels = np.array([18, -18])
    if k % 512:
        return np.exp2(np.random.permutation(np.resize(levels, k // 32))).repeat(32)
    a = np.empty((k // 512, 16))
    for p in range(k // 512):
        a[p, :8] = np.random.permutation(np.resize(levels, 8))
        for g in range(8):
            far = levels[np.abs(levels - a[p, g]) >= 10]
            a[p, g + 8] = far[np.random.randint(len(far))]
    return np.exp2(a.ravel()).repeat(32)


def f64(x):
    return np.asarray(x).astype(np.float64)


def striped(idx):
    return np.tile(np.asarray(idx).reshape(-1, 16).T, (8, 1)).astype(np.uint16)


def unstriped(offs):
    return offs[:16].T.reshape(-1).astype(np.int64)


B, N, T, D, R = 1, 512, 2048, 512, 512


def setup_inputs():
    n = np.random.standard_normal
    idx = np.random.permutation(T)[:B * N]
    s = mx_kscale(D)[:, None]
    z = mx_kscale(R)[:, None]
    u = np.ones(T)
    u[idx] = mx_kscale(B * N)
    r = np.random.uniform(0.5, 2.0, T) * u
    x = n((B, D, R))
    return {
        "xT": (x * s).astype(np.float32),
        "wT": (n((D, T)) * (1.00 / np.sqrt(D)) / s / r).astype(np.float32),
        "y": np.random.randint(0, 2, (B, R, N)).astype(np.float32),
        "wt": (np.random.uniform(0.5, 1.5, (B, R, 1)) * 1.0 / np.sqrt(R) * z).astype(np.float32),
        "ts": np.tile(r, (128, 1)).astype(np.float32),
        "xm": (x.transpose(0, 2, 1) / z).astype(np.float32),
        "offs": striped(idx),
    }


def reference(xT, wT, y, wt, ts, xm, offs):
    idx = unstriped(offs)
    pick = lambda x: x[:, idx].reshape(x.shape[0], B, N).transpose(1, 0, 2)
    w = pick(f64(wT))
    a = mxq(f64(xT), 1, "e4m3").transpose(0, 2, 1) @ mxq(w, 1, "e4m3")
    ts_ = pick(f64(ts))[:, :1, :]
    a = a * ts_
    g = f64(wt) * (1.0 / (1.0 + np.exp(-a)) - f64(y))
    g = g * ts_
    dw = mxq(f64(xm), 1, "e4m3").transpose(0, 2, 1) @ mxq(g, 1, "e5m2")
    gw = np.zeros((D, T))
    gw[:, idx] = dw.transpose(1, 0, 2).reshape(D, B * N)
    gx = mxq(g, 2, "e5m2") @ mxq(w, 2, "e4m3").transpose(0, 2, 1)
    return gw, gx

@@ -1,0 +1,202 @@
+from contextlib import ExitStack
+
+import concourse.mybir as mybir
+from concourse.masks import make_identity
+
+N, T, D, R = 512, 2048, 512, 512
+FLOPS = 3 * 2 * N * D * R
+
+F32 = mybir.dt.float32
+BF16 = mybir.dt.bfloat16
+U32 = mybir.dt.uint32
+U16 = mybir.dt.uint16
+U8 = mybir.dt.uint8
+E4M3 = mybir.dt.float8_e4m3fn_x4
+E5M2 = mybir.dt.float8_e5m2_x4
+ALU = mybir.AluOpType
+ACT = mybir.ActivationFunctionType
+
+P = 128
+PACK = 4
+HALF = R // 2
+
+
+def tile_attend_gnce_wx_ts_kernel(tc, xT, wT, y, wt, ts, xm, offs, out_0, out_1):
+    nc = tc.nc
+    with ExitStack() as ctx:
+        sb = ctx.enter_context(tc.tile_pool(name="sb", bufs=1))
+        ps = ctx.enter_context(tc.psum_pool(name="ps", bufs=1))
+
+        def mx_tiles(name, width):
+            codes = sb.tile([P, width], U32, name=name + "_codes", align_bytes=64)
+            scales = sb.tile([P, width], U8, name=name + "_scales", align_bytes=64)
+            return codes, scales
+
+        def quantise(operand, cols, values, fmt):
+            codes, scales = operand
+            nc.vector.quantize_mx(out=codes[:, cols].bitcast(fmt), scales=scales[:, cols], in_=values)
+
+        def product(out, stationary, s_cols, s_fmt, moving, m_fmt):
+            nc.tensor.matmul_mx(
+                out=out,
+                lhsT=stationary[0][:, s_cols].bitcast(s_fmt),
+                lhsT_scale=stationary[1][:, s_cols],
+                rhs=moving[0][:].bitcast(m_fmt),
+                rhs_scale=moving[1][:],
+                start=True,
+                stop=True,
+            )
+
+        banks = [ps.tile([P, 512], F32, name="bank%d" % b) for b in range(8)]
+
+        offsets = sb.tile([P, N // 16], U16, name="offsets")
+        nc.sync.dma_start(offsets[:], offs)
+        planes = []
+        w_rows = wT.rearrange("(p j) c -> p j c", j=PACK)
+        for j in range(PACK):
+            plane = sb.tile([P, T], F32, name="w_plane%d" % j)
+            nc.sync.dma_start(plane[:], w_rows[:, j, :])
+            planes.append(plane)
+        y_half, x_half = [], []
+        x_rows = xT[0].rearrange("(p j) r -> p j r", j=PACK)
+        y_rows = y[0].rearrange("(c p) i -> p c i", p=P)
+        for h in range(2):
+            xt = sb.tile([P, PACK, HALF], F32, name="x_half%d" % h)
+            nc.sync.dma_start(xt[:], x_rows[:, :, HALF * h : HALF * (h + 1)])
+            x_half.append(xt)
+            yt = sb.tile([P, 2, N], F32, name="y_half%d" % h)
+            nc.sync.dma_start(yt[:], y_rows[:, 2 * h : 2 * h + 2, :])
+            y_half.append(yt)
+        xm_raw = sb.tile([P, PACK, D], F32, name="xm_raw")
+        nc.sync.dma_start(xm_raw[:], xm[0].rearrange("(p j) d -> p j d", j=PACK))
+
+        wt_cols = sb.tile([P, PACK], F32, name="wt_cols")
+        nc.scalar.dma_start(wt_cols[:], wt[0].rearrange("(p c) o -> p (c o)", c=PACK))
+        ts_window = sb.tile([P, T], F32, name="ts_window")
+        nc.vector.memset(ts_window[:], 0.0)
+        nc.scalar.dma_start(ts_window[0:1, :], ts[0:1, :])
+
+        identity = sb.tile([P, P], F32, name="identity")
+        make_identity(nc, identity[:])
+        warm = sb.tile([P, 1], F32, name="warm")
+        nc.scalar.activation(warm[:], identity[:, 0:1], ACT.Sigmoid)
+
+        windows = []
+        for c in range(D // P):
+            window = sb.tile([P, T], F32, name="window%d" % c)
+            nc.gpsimd.memset(window[:], 0.0)
+            windows.append(window)
+
+        ts_listed = sb.tile([P, N], F32, name="ts_listed")
+        nc.vector.tensor_copy(ts_listed[:], ts_window[:].indirect(offsets[:]))
+        for t in range(PACK):
+            nc.tensor.transpose(banks[7][:, P * t : P * (t + 1)], ts_listed[:, t:N:PACK], identity[:])
+        ts_cols = sb.tile([P, PACK], F32, name="ts_cols")
+        nc.scalar.copy(ts_cols[:], banks[7][:, 0:512:P])
+        for c in range(PACK):
+            nc.tensor.transpose(banks[6][:, P * c : P * (c + 1)], wt_cols[:, c : c + 1].to_broadcast([P, P]), identity[:])
+        coef = sb.tile([P, 2, PACK, HALF], F32, name="coef")
+        for t in range(PACK):
+            nc.scalar.activation(
+                coef[:, :, t, :].rearrange("p h (n c) -> p h n c", c=PACK),
+                banks[6][:].rearrange("p (c h n) -> p h n c", c=PACK, h=2),
+                ACT.Copy,
+                scale=ts_cols[:, t : t + 1],
+            )
+
+        w_d = sb.tile([P, PACK, P, PACK], BF16, name="w_d", align_bytes=64)
+        w_words = w_d[:].rearrange("p t s j -> p (t s j)").bitcast(F32)
+        w_i = sb.tile([P, 2, P, 2, PACK], BF16, name="w_i", align_bytes=64)
+        wd_mx = mx_tiles("wd", N)
+        for u in range(2):
+            for j in (2 * u, 2 * u + 1):
+                nc.vector.tensor_copy(w_d[:].rearrange("p t s j -> p s t j")[:, :, :, j], planes[j][:].indirect(offsets[:]))
+            if u == 1:
+                quantise(wd_mx, slice(0, N), w_d[:].rearrange("p t s j -> p (t s j)"), E4M3)
+            bank = banks[4 + 3 * u]
+            for t in range(PACK):
+                nc.tensor.transpose(bank[:, P * t : P * (t + 1)], w_words[:, 2 * P * t + u : 2 * P * (t + 1) : 2], identity[:])
+            nc.scalar.copy(w_i[:, u, :, :, :], bank[:].bitcast(BF16).rearrange("s (t p e) -> s p e t", t=PACK, e=2))
+
+        h_all = sb.tile([P, PACK * R], BF16, name="h_all", align_bytes=64)
+        h_tiles = h_all[:].rearrange("s (t r) -> s t r", t=PACK)
+        x_mxs = []
+        for h in range(2):
+            x_d = sb.tile([P, HALF, PACK], BF16, name="x_d%d" % h, align_bytes=64)
+            interleave = nc.scalar.copy if h == 0 else nc.vector.tensor_copy
+            interleave(x_d[:], x_half[h][:].rearrange("p j r -> p r j"))
+            x_mxs.append(mx_tiles("x%d" % h, HALF))
+            quantise(x_mxs[h], slice(0, HALF), x_d[:].rearrange("p r j -> p (r j)"), E4M3)
+        for h in range(2):
+            x_mx = x_mxs[h]
+            sig, diff = [], []
+            for q in range(2):
+                sg = sb.tile([P, 2, HALF], F32, name="sig%d%d" % (h, q))
+                for k in range(2):
+                    t = 2 * q + k
+                    scores = banks[4 + 2 * h + q][:, HALF * k : HALF * (k + 1)]
+                    product(scores, wd_mx, slice(P * t, P * (t + 1)), E4M3, x_mx, E4M3)
+                for k in range(2):
+                    t = 2 * q + k
+                    scores = banks[4 + 2 * h + q][:, HALF * k : HALF * (k + 1)]
+                    nc.scalar.activation(sg[:, k, :], scores, ACT.Sigmoid, scale=ts_cols[:, t : t + 1])
+                sig.append(sg)
+                for k in range(2):
+                    for c in range(2):
+                        nc.tensor.transpose(
+                            banks[2 * h + q][:, HALF * k + P * c : HALF * k + P * (c + 1)],
+                            y_half[h][:, c, 2 * q + k : N : PACK],
+                            identity[:],
+                        )
+            for q in range(2):
+                df = sb.tile([P, 2, HALF], F32, name="diff%d%d" % (h, q))
+                nc.vector.tensor_tensor(df[:].rearrange("p k r -> p (k r)"), sig[q][:].rearrange("p k r -> p (k r)"), banks[2 * h + q][:], ALU.subtract)
+                diff.append(df)
+            if h == 0:
+                for q in range(2):
+                    nc.vector.tensor_tensor(h_tiles[:, 2 * q : 2 * q + 2, 0:HALF], diff[q][:], coef[:, h, 2 * q : 2 * q + 2, :], ALU.mult)
+            else:
+                for t in range(PACK):
+                    nc.vector.tensor_tensor(h_tiles[:, t, HALF:R], diff[t // 2][:, t % 2, :], coef[:, h, t, :], ALU.mult)
+
+        xm_mx = mx_tiles("xm", D)
+
+        def prepare_xm(c):
+            xm_r = sb.tile([P, P, PACK], BF16, name="xm_r%d" % c, align_bytes=64)
+            nc.scalar.copy(xm_r[:], xm_raw[:, :, P * c : P * (c + 1)].rearrange("p j d -> p d j"))
+            quantise(xm_mx, slice(P * c, P * (c + 1)), xm_r[:].rearrange("p d j -> p (d j)"), E4M3)
+
+        prepare_xm(0)
+        hr_mx = mx_tiles("hr", N)
+        turn_banks = [banks[0], banks[1], banks[4], banks[5]]
+        for t in range(PACK):
+            words = h_all[:, R * t : R * (t + 1)].bitcast(F32)
+            for u in range(2):
+                nc.tensor.transpose(turn_banks[t][:, P * u : P * (u + 1)], words[:, u:HALF:2], identity[:])
+            h_r = sb.tile([P, P, 2], F32, name="h_r%d" % t, align_bytes=64)
+            nc.scalar.copy(h_r[:], turn_banks[t][:, 0 : 2 * P].rearrange("p (u s) -> p s u", u=2))
+            quantise(hr_mx, slice(P * t, P * (t + 1)), h_r[:].rearrange("p s u -> p (s u)").bitcast(BF16), E5M2)
+
+        dw_banks = [banks[2], banks[3], banks[6], banks[7]]
+        for c in range(D // P):
+            product(dw_banks[c][:], xm_mx, slice(P * c, P * (c + 1)), E4M3, hr_mx, E5M2)
+            dw = sb.tile([P, P, PACK], F32, name="dw%d" % c)
+            nc.scalar.copy(dw[:], dw_banks[c][:].rearrange("p (t s) -> p s t", t=PACK))
+            nc.vector.tensor_copy(windows[c][:].indirect(offsets[:]), dw[:].rearrange("p s t -> p (s t)"))
+            nc.sync.dma_start(out_0[P * c : P * (c + 1), :], windows[c][:])
+            if c + 1 < D // P:
+                prepare_xm(c + 1)
+
+        wi_mx = mx_tiles("wi", D)
+        quantise(wi_mx, slice(0, D), w_i[:].rearrange("s u p e t -> s (u p e t)"), E4M3)
+        hi_mx = mx_tiles("hi", R)
+        for h in range(2):
+            h_i = sb.tile([P, HALF, PACK], BF16, name="h_i%d" % h, align_bytes=64)
+            interleave = nc.scalar.copy if h == 0 else nc.vector.tensor_copy
+            interleave(h_i[:], h_tiles[:, :, HALF * h : HALF * (h + 1)].rearrange("s t r -> s r t"))
+            quantise(hi_mx, slice(HALF * h, HALF * (h + 1)), h_i[:].rearrange("s r t -> s (r t)"), E5M2)
+        for c in range(R // P):
+            product(turn_banks[c][:], hi_mx, slice(P * c, P * (c + 1)), E5M2, wi_mx, E4M3)
+            gx = sb.tile([P, P, 2, 2], F32, name="gx%d" % c)
+            nc.scalar.copy(gx[:], turn_banks[c][:].rearrange("r (u p e) -> r p u e", u=2, e=2))
+            nc.scalar.dma_start(out_1[0, P * c : P * (c + 1), :], gx[:].rearrange("r p u e -> r (p u e)"))

@@ -28,8 +28,8 @@ def tile_attend_gnce_wx_ts_kernel(tc, xT, wT, y, wt, ts, xm, offs, out_0, out_1)
         ps = ctx.enter_context(tc.psum_pool(name="ps", bufs=1))
 
         def mx_tiles(name, width):
-            codes = sb.tile([P, width], U32, name=name + "_codes", align_bytes=64)
-            scales = sb.tile([P, width], U8, name=name + "_scales", align_bytes=64)
+            codes = sb.tile([P, width], U32, name=name + "_codes", tag=name + "_codes", align_bytes=64)
+            scales = sb.tile([P, width], U8, name=name + "_scales", tag=name + "_scales", align_bytes=64)
             return codes, scales
 
         def quantise(operand, cols, values, fmt):
@@ -49,6 +49,8 @@ def tile_attend_gnce_wx_ts_kernel(tc, xT, wT, y, wt, ts, xm, offs, out_0, out_1)
 
         banks = [ps.tile([P, 512], F32, name="bank%d" % b) for b in range(8)]
 
+        ts_row = sb.tile([1, T], F32, name="ts_row")
+        nc.sync.dma_start(ts_row[:], ts[0:1, :])
         offsets = sb.tile([P, N // 16], U16, name="offsets")
         nc.sync.dma_start(offsets[:], offs)
         planes = []
@@ -57,11 +59,14 @@ def tile_attend_gnce_wx_ts_kernel(tc, xT, wT, y, wt, ts, xm, offs, out_0, out_1)
             plane = sb.tile([P, T], F32, name="w_plane%d" % j)
             nc.sync.dma_start(plane[:], w_rows[:, j, :])
             planes.append(plane)
+            if j == 0:
+                wt_cols = sb.tile([P, PACK], F32, name="wt_cols")
+                nc.sync.dma_start(wt_cols[:], wt[0].rearrange("(p c) o -> p (c o)", c=PACK))
         y_half, x_half = [], []
         x_rows = xT[0].rearrange("(p j) r -> p j r", j=PACK)
         y_rows = y[0].rearrange("(c p) i -> p c i", p=P)
         for h in range(2):
-            xt = sb.tile([P, PACK, HALF], F32, name="x_half%d" % h)
+            xt = sb.tile([P, PACK, HALF], F32, name="x_half%d" % h, tag="x_half%d" % h, align_bytes=64)
             nc.sync.dma_start(xt[:], x_rows[:, :, HALF * h : HALF * (h + 1)])
             x_half.append(xt)
             yt = sb.tile([P, 2, N], F32, name="y_half%d" % h)
@@ -70,11 +75,9 @@ def tile_attend_gnce_wx_ts_kernel(tc, xT, wT, y, wt, ts, xm, offs, out_0, out_1)
         xm_raw = sb.tile([P, PACK, D], F32, name="xm_raw")
         nc.sync.dma_start(xm_raw[:], xm[0].rearrange("(p j) d -> p j d", j=PACK))
 
-        wt_cols = sb.tile([P, PACK], F32, name="wt_cols")
-        nc.scalar.dma_start(wt_cols[:], wt[0].rearrange("(p c) o -> p (c o)", c=PACK))
         ts_window = sb.tile([P, T], F32, name="ts_window")
         nc.vector.memset(ts_window[:], 0.0)
-        nc.scalar.dma_start(ts_window[0:1, :], ts[0:1, :])
+        nc.vector.tensor_copy(ts_window[0:1, :], ts_row[:])
 
         identity = sb.tile([P, P], F32, name="identity")
         make_identity(nc, identity[:])
@@ -91,7 +94,7 @@ def tile_attend_gnce_wx_ts_kernel(tc, xT, wT, y, wt, ts, xm, offs, out_0, out_1)
         nc.vector.tensor_copy(ts_listed[:], ts_window[:].indirect(offsets[:]))
         for t in range(PACK):
             nc.tensor.transpose(banks[7][:, P * t : P * (t + 1)], ts_listed[:, t:N:PACK], identity[:])
-        ts_cols = sb.tile([P, PACK], F32, name="ts_cols")
+        ts_cols = sb.tile([P, PACK], F32, name="ts_cols", tag="ts_cols", align_bytes=64)
         nc.scalar.copy(ts_cols[:], banks[7][:, 0:512:P])
         for c in range(PACK):
             nc.tensor.transpose(banks[6][:, P * c : P * (c + 1)], wt_cols[:, c : c + 1].to_broadcast([P, P]), identity[:])
@@ -106,27 +109,37 @@ def tile_attend_gnce_wx_ts_kernel(tc, xT, wT, y, wt, ts, xm, offs, out_0, out_1)
 
         w_d = sb.tile([P, PACK, P, PACK], BF16, name="w_d", align_bytes=64)
         w_words = w_d[:].rearrange("p t s j -> p (t s j)").bitcast(F32)
-        w_i = sb.tile([P, 2, P, 2, PACK], BF16, name="w_i", align_bytes=64)
+        wi_mx = mx_tiles("wi", D)
         wd_mx = mx_tiles("wd", N)
-        for u in range(2):
-            for j in (2 * u, 2 * u + 1):
-                nc.vector.tensor_copy(w_d[:].rearrange("p t s j -> p s t j")[:, :, :, j], planes[j][:].indirect(offsets[:]))
-            if u == 1:
-                quantise(wd_mx, slice(0, N), w_d[:].rearrange("p t s j -> p (t s j)"), E4M3)
-            bank = banks[4 + 3 * u]
+
+        def turn_w(u, bank, tag):
             for t in range(PACK):
                 nc.tensor.transpose(bank[:, P * t : P * (t + 1)], w_words[:, 2 * P * t + u : 2 * P * (t + 1) : 2], identity[:])
-            nc.scalar.copy(w_i[:, u, :, :, :], bank[:].bitcast(BF16).rearrange("s (t p e) -> s p e t", t=PACK, e=2))
+            w_i = sb.tile([P, P, 2, PACK], BF16, name="w_i%d" % u, tag=tag, align_bytes=64)
+            nc.scalar.copy(w_i[:], bank[:].bitcast(BF16).rearrange("s (t p e) -> s p e t", t=PACK, e=2))
+            return w_i
 
-        h_all = sb.tile([P, PACK * R], BF16, name="h_all", align_bytes=64)
+        def quantise_w_i(u, w_i):
+            quantise(wi_mx, slice(HALF * u, HALF * (u + 1)), w_i[:].rearrange("s p e t -> s (p e t)"), E4M3)
+
+        for j in range(PACK):
+            nc.vector.tensor_copy(w_d[:].rearrange("p t s j -> p s t j")[:, :, :, j], planes[j][:].indirect(offsets[:]))
+            if j == 1:
+                quantise_w_i(0, turn_w(0, banks[0], "w_i0"))
+        quantise(wd_mx, slice(0, N), w_d[:].rearrange("p t s j -> p (t s j)"), E4M3)
+
+        h_all = sb.tile([P, PACK * R], BF16, name="h_all", tag="h_all", align_bytes=64)
         h_tiles = h_all[:].rearrange("s (t r) -> s t r", t=PACK)
         x_mxs = []
         for h in range(2):
-            x_d = sb.tile([P, HALF, PACK], BF16, name="x_d%d" % h, align_bytes=64)
+            x_d = sb.tile([P, HALF, PACK], BF16, name="x_d%d" % h, tag="x_d", align_bytes=64)
             interleave = nc.scalar.copy if h == 0 else nc.vector.tensor_copy
             interleave(x_d[:], x_half[h][:].rearrange("p j r -> p r j"))
             x_mxs.append(mx_tiles("x%d" % h, HALF))
             quantise(x_mxs[h], slice(0, HALF), x_d[:].rearrange("p r j -> p (r j)"), E4M3)
+        w_i1 = turn_w(1, banks[1], "x_half0")
+        score_banks = [[banks[4], banks[5]], [banks[2], banks[3]]]
+        y_banks = [[banks[0], banks[1]], [banks[4], banks[5]]]
         for h in range(2):
             x_mx = x_mxs[h]
             sig, diff = [], []
@@ -134,23 +147,23 @@ def tile_attend_gnce_wx_ts_kernel(tc, xT, wT, y, wt, ts, xm, offs, out_0, out_1)
                 sg = sb.tile([P, 2, HALF], F32, name="sig%d%d" % (h, q))
                 for k in range(2):
                     t = 2 * q + k
-                    scores = banks[4 + 2 * h + q][:, HALF * k : HALF * (k + 1)]
+                    scores = score_banks[h][q][:, HALF * k : HALF * (k + 1)]
                     product(scores, wd_mx, slice(P * t, P * (t + 1)), E4M3, x_mx, E4M3)
                 for k in range(2):
                     t = 2 * q + k
-                    scores = banks[4 + 2 * h + q][:, HALF * k : HALF * (k + 1)]
+                    scores = score_banks[h][q][:, HALF * k : HALF * (k + 1)]
                     nc.scalar.activation(sg[:, k, :], scores, ACT.Sigmoid, scale=ts_cols[:, t : t + 1])
                 sig.append(sg)
                 for k in range(2):
                     for c in range(2):
                         nc.tensor.transpose(
-                            banks[2 * h + q][:, HALF * k + P * c : HALF * k + P * (c + 1)],
+                            y_banks[h][q][:, HALF * k + P * c : HALF * k + P * (c + 1)],
                             y_half[h][:, c, 2 * q + k : N : PACK],
                             identity[:],
                         )
             for q in range(2):
                 df = sb.tile([P, 2, HALF], F32, name="diff%d%d" % (h, q))
-                nc.vector.tensor_tensor(df[:].rearrange("p k r -> p (k r)"), sig[q][:].rearrange("p k r -> p (k r)"), banks[2 * h + q][:], ALU.subtract)
+                nc.vector.tensor_tensor(df[:].rearrange("p k r -> p (k r)"), sig[q][:].rearrange("p k r -> p (k r)"), y_banks[h][q][:], ALU.subtract)
                 diff.append(df)
             if h == 0:
                 for q in range(2):
@@ -159,16 +172,15 @@ def tile_attend_gnce_wx_ts_kernel(tc, xT, wT, y, wt, ts, xm, offs, out_0, out_1)
                 for t in range(PACK):
                     nc.vector.tensor_tensor(h_tiles[:, t, HALF:R], diff[t // 2][:, t % 2, :], coef[:, h, t, :], ALU.mult)
 
-        xm_mx = mx_tiles("xm", D)
+        def prepare_xm(half, tag):
+            xm_r = sb.tile([P, HALF, PACK], BF16, name="xm_r%d" % half, tag=tag, align_bytes=64)
+            nc.scalar.copy(xm_r[:], xm_raw[:, :, HALF * half : HALF * (half + 1)].rearrange("p j d -> p d j"))
+            xm_mx = mx_tiles("xm%d" % half, HALF)
+            quantise(xm_mx, slice(0, HALF), xm_r[:].rearrange("p d j -> p (d j)"), E4M3)
+            return xm_mx
 
-        def prepare_xm(c):
-            xm_r = sb.tile([P, P, PACK], BF16, name="xm_r%d" % c, align_bytes=64)
-            nc.scalar.copy(xm_r[:], xm_raw[:, :, P * c : P * (c + 1)].rearrange("p j d -> p d j"))
-            quantise(xm_mx, slice(P * c, P * (c + 1)), xm_r[:].rearrange("p d j -> p (d j)"), E4M3)
-
-        prepare_xm(0)
         hr_mx = mx_tiles("hr", N)
-        turn_banks = [banks[0], banks[1], banks[4], banks[5]]
+        turn_banks = [banks[0], banks[1], banks[6], banks[7]]
         for t in range(PACK):
             words = h_all[:, R * t : R * (t + 1)].bitcast(F32)
             for u in range(2):
@@ -176,27 +188,38 @@ def tile_attend_gnce_wx_ts_kernel(tc, xT, wT, y, wt, ts, xm, offs, out_0, out_1)
             h_r = sb.tile([P, P, 2], F32, name="h_r%d" % t, align_bytes=64)
             nc.scalar.copy(h_r[:], turn_banks[t][:, 0 : 2 * P].rearrange("p (u s) -> p s u", u=2))
             quantise(hr_mx, slice(P * t, P * (t + 1)), h_r[:].rearrange("p s u -> p (s u)").bitcast(BF16), E5M2)
+        xm_low = prepare_xm(0, "ts_cols")
+        quantise_w_i(1, w_i1)
 
-        dw_banks = [banks[2], banks[3], banks[6], banks[7]]
-        for c in range(D // P):
-            product(dw_banks[c][:], xm_mx, slice(P * c, P * (c + 1)), E4M3, hr_mx, E5M2)
-            dw = sb.tile([P, P, PACK], F32, name="dw%d" % c)
-            nc.scalar.copy(dw[:], dw_banks[c][:].rearrange("p (t s) -> p s t", t=PACK))
-            nc.vector.tensor_copy(windows[c][:].indirect(offsets[:]), dw[:].rearrange("p s t -> p (s t)"))
+        dw_banks = [banks[2], banks[3], banks[4], banks[5]]
+
+        def dw_products(half, xm_mx):
+            for k in range(2):
+                product(dw_banks[2 * half + k][:], xm_mx, slice(P * k, P * (k + 1)), E4M3, hr_mx, E5M2)
+
+        def scatter(c, dw):
+            nc.scalar.copy(dw.rearrange("p (s t) -> p s t", t=PACK), dw_banks[c][:].rearrange("p (t s) -> p s t", t=PACK))
+            nc.vector.tensor_copy(windows[c][:].indirect(offsets[:]), dw)
             nc.sync.dma_start(out_0[P * c : P * (c + 1), :], windows[c][:])
-            if c + 1 < D // P:
-                prepare_xm(c + 1)
 
-        wi_mx = mx_tiles("wi", D)
-        quantise(wi_mx, slice(0, D), w_i[:].rearrange("s u p e t -> s (u p e t)"), E4M3)
+        dw_products(0, xm_low)
+        dw0 = sb.tile([P, N], F32, name="dw0")
+        scatter(0, dw0[:])
+        xm_high = prepare_xm(1, "xm0_scales")
+        dw1 = sb.tile([P, N], F32, name="dw1")
+        scatter(1, dw1[:])
+        dw_products(1, xm_high)
+
         hi_mx = mx_tiles("hi", R)
-        for h in range(2):
-            h_i = sb.tile([P, HALF, PACK], BF16, name="h_i%d" % h, align_bytes=64)
-            interleave = nc.scalar.copy if h == 0 else nc.vector.tensor_copy
-            interleave(h_i[:], h_tiles[:, :, HALF * h : HALF * (h + 1)].rearrange("s t r -> s r t"))
-            quantise(hi_mx, slice(HALF * h, HALF * (h + 1)), h_i[:].rearrange("s r t -> s (r t)"), E5M2)
+        h_i = sb.tile([P, R, PACK], BF16, name="h_i", tag="xm0_codes", align_bytes=64)
+        nc.scalar.copy(h_i[:], h_tiles.rearrange("s t r -> s r t"))
+        quantise(hi_mx, slice(0, R), h_i[:].rearrange("s r t -> s (r t)"), E5M2)
+        dw23 = sb.tile([P, 2 * N], F32, name="dw23", tag="h_all", align_bytes=64)
+        scatter(2, dw23[:, 0:N])
+        scatter(3, dw23[:, N : 2 * N])
+        gx_banks = [banks[2], banks[3], banks[0], banks[1]]
         for c in range(R // P):
-            product(turn_banks[c][:], hi_mx, slice(P * c, P * (c + 1)), E5M2, wi_mx, E4M3)
+            product(gx_banks[c][:], hi_mx, slice(P * c, P * (c + 1)), E5M2, wi_mx, E4M3)
             gx = sb.tile([P, P, 2, 2], F32, name="gx%d" % c)
-            nc.scalar.copy(gx[:], turn_banks[c][:].rearrange("r (u p e) -> r p u e", u=2, e=2))
+            nc.scalar.copy(gx[:], gx_banks[c][:].rearrange("r (u p e) -> r p u e", u=2, e=2))
             nc.scalar.dma_start(out_1[0, P * c : P * (c + 1), :], gx[:].rearrange("r p u e -> r (p u e)"))

@@ -8,6 +8,7 @@ FLOPS = 3 * 2 * N * D * R
 
 F32 = mybir.dt.float32
 BF16 = mybir.dt.bfloat16
+I32 = mybir.dt.int32
 U32 = mybir.dt.uint32
 U16 = mybir.dt.uint16
 U8 = mybir.dt.uint8
@@ -76,29 +77,29 @@ def tile_attend_gnce_wx_ts_kernel(tc, xT, wT, y, wt, ts, xm, offs, out_0, out_1)
         nc.sync.dma_start(xm_raw[:], xm[0].rearrange("(p j) d -> p j d", j=PACK))
 
         ts_window = sb.tile([P, T], F32, name="ts_window")
-        nc.vector.memset(ts_window[:], 0.0)
-        nc.vector.tensor_copy(ts_window[0:1, :], ts_row[:])
+        nc.vector.memset(ts_window[:].bitcast(I32), 0)
 
         identity = sb.tile([P, P], F32, name="identity")
         make_identity(nc, identity[:])
         warm = sb.tile([P, 1], F32, name="warm")
         nc.scalar.activation(warm[:], identity[:, 0:1], ACT.Sigmoid)
 
+        nc.scalar.copy(ts_window[0:1, :], ts_row[:])
         windows = []
-        for c in range(D // P):
+        for c in range(2):
             window = sb.tile([P, T], F32, name="window%d" % c)
-            nc.gpsimd.memset(window[:], 0.0)
+            nc.vector.memset(window[:].bitcast(I32), 0)
             windows.append(window)
 
         ts_listed = sb.tile([P, N], F32, name="ts_listed")
         nc.vector.tensor_copy(ts_listed[:], ts_window[:].indirect(offsets[:]))
         for t in range(PACK):
-            nc.tensor.transpose(banks[7][:, P * t : P * (t + 1)], ts_listed[:, t:N:PACK], identity[:])
+            nc.tensor.transpose(banks[7][:, P * t : P * (t + 1)], ts_listed[:, P * t : P * (t + 1)], identity[:])
         ts_cols = sb.tile([P, PACK], F32, name="ts_cols", tag="ts_cols", align_bytes=64)
         nc.scalar.copy(ts_cols[:], banks[7][:, 0:512:P])
         for c in range(PACK):
             nc.tensor.transpose(banks[6][:, P * c : P * (c + 1)], wt_cols[:, c : c + 1].to_broadcast([P, P]), identity[:])
-        coef = sb.tile([P, 2, PACK, HALF], F32, name="coef")
+        coef = sb.tile([P, 2, PACK, HALF], F32, name="coef", tag="coef", align_bytes=64)
         for t in range(PACK):
             nc.scalar.activation(
                 coef[:, :, t, :].rearrange("p h (n c) -> p h n c", c=PACK),
@@ -107,14 +108,14 @@ def tile_attend_gnce_wx_ts_kernel(tc, xT, wT, y, wt, ts, xm, offs, out_0, out_1)
                 scale=ts_cols[:, t : t + 1],
             )
 
-        w_d = sb.tile([P, PACK, P, PACK], BF16, name="w_d", align_bytes=64)
-        w_words = w_d[:].rearrange("p t s j -> p (t s j)").bitcast(F32)
+        w_d = sb.tile([P, N, PACK], BF16, name="w_d", align_bytes=64)
+        w_words = w_d[:].rearrange("p i j -> p (i j)").bitcast(F32)
         wi_mx = mx_tiles("wi", D)
         wd_mx = mx_tiles("wd", N)
 
         def turn_w(u, bank, tag):
             for t in range(PACK):
-                nc.tensor.transpose(bank[:, P * t : P * (t + 1)], w_words[:, 2 * P * t + u : 2 * P * (t + 1) : 2], identity[:])
+                nc.tensor.transpose(bank[:, P * t : P * (t + 1)], w_words[:, 2 * t + u : 2 * N : 2 * PACK], identity[:])
             w_i = sb.tile([P, P, 2, PACK], BF16, name="w_i%d" % u, tag=tag, align_bytes=64)
             nc.scalar.copy(w_i[:], bank[:].bitcast(BF16).rearrange("s (t p e) -> s p e t", t=PACK, e=2))
             return w_i
@@ -123,10 +124,8 @@ def tile_attend_gnce_wx_ts_kernel(tc, xT, wT, y, wt, ts, xm, offs, out_0, out_1)
             quantise(wi_mx, slice(HALF * u, HALF * (u + 1)), w_i[:].rearrange("s p e t -> s (p e t)"), E4M3)
 
         for j in range(PACK):
-            nc.vector.tensor_copy(w_d[:].rearrange("p t s j -> p s t j")[:, :, :, j], planes[j][:].indirect(offsets[:]))
-            if j == 1:
-                quantise_w_i(0, turn_w(0, banks[0], "w_i0"))
-        quantise(wd_mx, slice(0, N), w_d[:].rearrange("p t s j -> p (t s j)"), E4M3)
+            nc.vector.tensor_copy(w_d[:, :, j], planes[j][:].indirect(offsets[:]))
+        quantise(wd_mx, slice(0, N), w_d[:].rearrange("p i j -> p (i j)"), E4M3)
 
         h_all = sb.tile([P, PACK * R], BF16, name="h_all", tag="h_all", align_bytes=64)
         h_tiles = h_all[:].rearrange("s (t r) -> s t r", t=PACK)
@@ -137,7 +136,7 @@ def tile_attend_gnce_wx_ts_kernel(tc, xT, wT, y, wt, ts, xm, offs, out_0, out_1)
             interleave(x_d[:], x_half[h][:].rearrange("p j r -> p r j"))
             x_mxs.append(mx_tiles("x%d" % h, HALF))
             quantise(x_mxs[h], slice(0, HALF), x_d[:].rearrange("p r j -> p (r j)"), E4M3)
-        w_i1 = turn_w(1, banks[1], "x_half0")
+        w_i0 = turn_w(0, banks[1], "x_half0")
         score_banks = [[banks[4], banks[5]], [banks[2], banks[3]]]
         y_banks = [[banks[0], banks[1]], [banks[4], banks[5]]]
         for h in range(2):
@@ -158,7 +157,7 @@ def tile_attend_gnce_wx_ts_kernel(tc, xT, wT, y, wt, ts, xm, offs, out_0, out_1)
                     for c in range(2):
                         nc.tensor.transpose(
                             y_banks[h][q][:, HALF * k + P * c : HALF * k + P * (c + 1)],
-                            y_half[h][:, c, 2 * q + k : N : PACK],
+                            y_half[h][:, c, P * (2 * q + k) : P * (2 * q + k + 1)],
                             identity[:],
                         )
             for q in range(2):
@@ -172,52 +171,59 @@ def tile_attend_gnce_wx_ts_kernel(tc, xT, wT, y, wt, ts, xm, offs, out_0, out_1)
                 for t in range(PACK):
                     nc.vector.tensor_tensor(h_tiles[:, t, HALF:R], diff[t // 2][:, t % 2, :], coef[:, h, t, :], ALU.mult)
 
-        def prepare_xm(half, tag):
+        def prepare_xm(half, tag, interleave):
             xm_r = sb.tile([P, HALF, PACK], BF16, name="xm_r%d" % half, tag=tag, align_bytes=64)
-            nc.scalar.copy(xm_r[:], xm_raw[:, :, HALF * half : HALF * (half + 1)].rearrange("p j d -> p d j"))
+            interleave(xm_r[:], xm_raw[:, :, HALF * half : HALF * (half + 1)].rearrange("p j d -> p d j"))
             xm_mx = mx_tiles("xm%d" % half, HALF)
             quantise(xm_mx, slice(0, HALF), xm_r[:].rearrange("p d j -> p (d j)"), E4M3)
             return xm_mx
 
         hr_mx = mx_tiles("hr", N)
         turn_banks = [banks[0], banks[1], banks[6], banks[7]]
+        h_r = sb.tile([P, 2 * N], F32, name="h_r", tag="h_r", align_bytes=64)
         for t in range(PACK):
             words = h_all[:, R * t : R * (t + 1)].bitcast(F32)
             for u in range(2):
                 nc.tensor.transpose(turn_banks[t][:, P * u : P * (u + 1)], words[:, u:HALF:2], identity[:])
-            h_r = sb.tile([P, P, 2], F32, name="h_r%d" % t, align_bytes=64)
-            nc.scalar.copy(h_r[:], turn_banks[t][:, 0 : 2 * P].rearrange("p (u s) -> p s u", u=2))
-            quantise(hr_mx, slice(P * t, P * (t + 1)), h_r[:].rearrange("p s u -> p (s u)").bitcast(BF16), E5M2)
-        xm_low = prepare_xm(0, "ts_cols")
-        quantise_w_i(1, w_i1)
+            part = h_r[:, 2 * P * t : 2 * P * (t + 1)]
+            nc.scalar.copy(part.rearrange("p (s u) -> p s u", u=2), turn_banks[t][:, 0 : 2 * P].rearrange("p (u s) -> p s u", u=2))
+            quantise(hr_mx, slice(P * t, P * (t + 1)), part.bitcast(BF16), E5M2)
+        xm_low = prepare_xm(0, "ts_cols", nc.scalar.copy)
+        quantise_w_i(0, w_i0)
+        xm_high = prepare_xm(1, "coef", nc.vector.tensor_copy)
 
-        dw_banks = [banks[2], banks[3], banks[4], banks[5]]
+        dw_banks = [banks[3], banks[4], banks[5], banks[0]]
 
         def dw_products(half, xm_mx):
             for k in range(2):
                 product(dw_banks[2 * half + k][:], xm_mx, slice(P * k, P * (k + 1)), E4M3, hr_mx, E5M2)
 
         def scatter(c, dw):
-            nc.scalar.copy(dw.rearrange("p (s t) -> p s t", t=PACK), dw_banks[c][:].rearrange("p (t s) -> p s t", t=PACK))
-            nc.vector.tensor_copy(windows[c][:].indirect(offsets[:]), dw)
-            nc.sync.dma_start(out_0[P * c : P * (c + 1), :], windows[c][:])
+            nc.scalar.copy(dw, dw_banks[c][:])
+            nc.vector.tensor_copy(windows[c % 2][:].indirect(offsets[:]), dw)
+            nc.sync.dma_start(out_0[P * c : P * (c + 1), :], windows[c % 2][:])
 
         dw_products(0, xm_low)
-        dw0 = sb.tile([P, N], F32, name="dw0")
-        scatter(0, dw0[:])
-        xm_high = prepare_xm(1, "xm0_scales")
-        dw1 = sb.tile([P, N], F32, name="dw1")
-        scatter(1, dw1[:])
         dw_products(1, xm_high)
+        for c in range(2):
+            dw = sb.tile([P, N], F32, name="dw%d" % c)
+            scatter(c, dw[:])
 
+        quantise_w_i(1, turn_w(1, banks[2], "xm0_codes"))
         hi_mx = mx_tiles("hi", R)
-        h_i = sb.tile([P, R, PACK], BF16, name="h_i", tag="xm0_codes", align_bytes=64)
-        nc.scalar.copy(h_i[:], h_tiles.rearrange("s t r -> s r t"))
-        quantise(hi_mx, slice(0, R), h_i[:].rearrange("s r t -> s (r t)"), E5M2)
-        dw23 = sb.tile([P, 2 * N], F32, name="dw23", tag="h_all", align_bytes=64)
+        h_i = sb.tile([P, P, 2, 2 * PACK], BF16, name="h_i", align_bytes=64)
+        for u in range(2):
+            for t in range(PACK):
+                nc.tensor.transpose(dw_banks[u][:, P * t : P * (t + 1)], h_r[:, 2 * t + u : 2 * N : 2 * PACK], identity[:])
+            nc.scalar.copy(
+                h_i[:, :, u, :].rearrange("s p (e t) -> s p e t", e=2),
+                dw_banks[u][:].bitcast(BF16).rearrange("s (t p e) -> s p e t", t=PACK, e=2),
+            )
+        quantise(hi_mx, slice(0, R), h_i[:].rearrange("s p u x -> s (p u x)"), E5M2)
+        dw23 = sb.tile([P, 2 * N], F32, name="dw23", tag="h_r", align_bytes=64)
         scatter(2, dw23[:, 0:N])
         scatter(3, dw23[:, N : 2 * N])
-        gx_banks = [banks[2], banks[3], banks[0], banks[1]]
+        gx_banks = [banks[6], banks[7], banks[1], banks[2]]
         for c in range(R // P):
             product(gx_banks[c][:], hi_mx, slice(P * c, P * (c + 1)), E5M2, wi_mx, E4M3)
             gx = sb.tile([P, P, 2, 2], F32, name="gx%d" % c)

@@ -37,13 +37,13 @@ def tile_attend_gnce_wx_ts_kernel(tc, xT, wT, y, wt, ts, xm, offs, out_0, out_1)
             codes, scales = operand
             nc.vector.quantize_mx(out=codes[:, cols].bitcast(fmt), scales=scales[:, cols], in_=values)
 
-        def product(out, stationary, s_cols, s_fmt, moving, m_fmt):
+        def product(out, stationary, s_cols, s_fmt, moving, m_cols, m_fmt):
             nc.tensor.matmul_mx(
                 out=out,
                 lhsT=stationary[0][:, s_cols].bitcast(s_fmt),
                 lhsT_scale=stationary[1][:, s_cols],
-                rhs=moving[0][:].bitcast(m_fmt),
-                rhs_scale=moving[1][:],
+                rhs=moving[0][:, m_cols].bitcast(m_fmt),
+                rhs_scale=moving[1][:, m_cols],
                 start=True,
                 stop=True,
             )
@@ -90,6 +90,10 @@ def tile_attend_gnce_wx_ts_kernel(tc, xT, wT, y, wt, ts, xm, offs, out_0, out_1)
             window = sb.tile([P, T], F32, name="window%d" % c)
             nc.vector.memset(window[:].bitcast(I32), 0)
             windows.append(window)
+
+        hr_mx = mx_tiles("hr", HALF + N)
+        nc.vector.memset(hr_mx[0][:, 0:HALF], 0)
+        nc.vector.memset(hr_mx[1][:, 0:HALF].bitcast(U32), 0)
 
         ts_listed = sb.tile([P, N], F32, name="ts_listed")
         nc.vector.tensor_copy(ts_listed[:], ts_window[:].indirect(offsets[:]))
@@ -139,20 +143,18 @@ def tile_attend_gnce_wx_ts_kernel(tc, xT, wT, y, wt, ts, xm, offs, out_0, out_1)
         w_i0 = turn_w(0, banks[1], "x_half0")
         score_banks = [[banks[4], banks[5]], [banks[2], banks[3]]]
         y_banks = [[banks[0], banks[1]], [banks[4], banks[5]]]
+        sig = {}
         for h in range(2):
-            x_mx = x_mxs[h]
-            sig, diff = [], []
             for q in range(2):
-                sg = sb.tile([P, 2, HALF], F32, name="sig%d%d" % (h, q))
+                sig[h, q] = sb.tile([P, 2, HALF], F32, name="sig%d%d" % (h, q))
                 for k in range(2):
                     t = 2 * q + k
-                    scores = score_banks[h][q][:, HALF * k : HALF * (k + 1)]
-                    product(scores, wd_mx, slice(P * t, P * (t + 1)), E4M3, x_mx, E4M3)
+                    product(score_banks[h][q][:, HALF * k : HALF * (k + 1)], wd_mx, slice(P * t, P * (t + 1)), E4M3, x_mxs[h], slice(0, HALF), E4M3)
                 for k in range(2):
                     t = 2 * q + k
-                    scores = score_banks[h][q][:, HALF * k : HALF * (k + 1)]
-                    nc.scalar.activation(sg[:, k, :], scores, ACT.Sigmoid, scale=ts_cols[:, t : t + 1])
-                sig.append(sg)
+                    nc.scalar.activation(
+                        sig[h, q][:, k, :], score_banks[h][q][:, HALF * k : HALF * (k + 1)], ACT.Sigmoid, scale=ts_cols[:, t : t + 1]
+                    )
                 for k in range(2):
                     for c in range(2):
                         nc.tensor.transpose(
@@ -160,54 +162,61 @@ def tile_attend_gnce_wx_ts_kernel(tc, xT, wT, y, wt, ts, xm, offs, out_0, out_1)
                             y_half[h][:, c, P * (2 * q + k) : P * (2 * q + k + 1)],
                             identity[:],
                         )
-            for q in range(2):
-                df = sb.tile([P, 2, HALF], F32, name="diff%d%d" % (h, q))
-                nc.vector.tensor_tensor(df[:].rearrange("p k r -> p (k r)"), sig[q][:].rearrange("p k r -> p (k r)"), y_banks[h][q][:], ALU.subtract)
-                diff.append(df)
-            if h == 0:
-                for q in range(2):
-                    nc.vector.tensor_tensor(h_tiles[:, 2 * q : 2 * q + 2, 0:HALF], diff[q][:], coef[:, h, 2 * q : 2 * q + 2, :], ALU.mult)
-            else:
-                for t in range(PACK):
-                    nc.vector.tensor_tensor(h_tiles[:, t, HALF:R], diff[t // 2][:, t % 2, :], coef[:, h, t, :], ALU.mult)
 
-        def prepare_xm(half, tag, interleave):
+        h_r = sb.tile([P, 2 * N], F32, name="h_r", tag="h_r", align_bytes=64)
+
+        def form_h(q, bank):
+            diff = []
+            for h in range(2):
+                df = sb.tile([P, 2 * HALF], F32, name="diff%d%d" % (h, q))
+                nc.vector.tensor_tensor(df[:], sig[h, q][:].rearrange("p k r -> p (k r)"), y_banks[h][q][:], ALU.subtract)
+                diff.append(df)
+            for h in range(2):
+                nc.vector.tensor_tensor(
+                    h_tiles[:, 2 * q : 2 * q + 2, HALF * h : HALF * (h + 1)],
+                    diff[h][:].rearrange("p (k r) -> p k r", k=2),
+                    coef[:, h, 2 * q : 2 * q + 2, :],
+                    ALU.mult,
+                )
+            words = h_all[:, 2 * R * q : 2 * R * (q + 1)].bitcast(F32)
+            for k in range(2):
+                for u in range(2):
+                    nc.tensor.transpose(bank[:, P * (2 * k + u) : P * (2 * k + u + 1)], words[:, HALF * k + u : HALF * (k + 1) : 2], identity[:])
+            part = h_r[:, N * q : N * (q + 1)]
+            nc.scalar.copy(part.rearrange("p (k s u) -> p k s u", k=2, u=2), bank[:].rearrange("p (k u s) -> p k s u", k=2, u=2))
+            quantise(hr_mx, slice(HALF * (q + 1), HALF * (q + 2)), part.bitcast(BF16), E5M2)
+
+        def prepare_xm(half, tag):
             xm_r = sb.tile([P, HALF, PACK], BF16, name="xm_r%d" % half, tag=tag, align_bytes=64)
-            interleave(xm_r[:], xm_raw[:, :, HALF * half : HALF * (half + 1)].rearrange("p j d -> p d j"))
+            nc.scalar.copy(xm_r[:], xm_raw[:, :, HALF * half : HALF * (half + 1)].rearrange("p j d -> p d j"))
             xm_mx = mx_tiles("xm%d" % half, HALF)
             quantise(xm_mx, slice(0, HALF), xm_r[:].rearrange("p d j -> p (d j)"), E4M3)
             return xm_mx
 
-        hr_mx = mx_tiles("hr", N)
-        turn_banks = [banks[0], banks[1], banks[6], banks[7]]
-        h_r = sb.tile([P, 2 * N], F32, name="h_r", tag="h_r", align_bytes=64)
-        for t in range(PACK):
-            words = h_all[:, R * t : R * (t + 1)].bitcast(F32)
-            for u in range(2):
-                nc.tensor.transpose(turn_banks[t][:, P * u : P * (u + 1)], words[:, u:HALF:2], identity[:])
-            part = h_r[:, 2 * P * t : 2 * P * (t + 1)]
-            nc.scalar.copy(part.rearrange("p (s u) -> p s u", u=2), turn_banks[t][:, 0 : 2 * P].rearrange("p (u s) -> p s u", u=2))
-            quantise(hr_mx, slice(P * t, P * (t + 1)), part.bitcast(BF16), E5M2)
-        xm_low = prepare_xm(0, "ts_cols", nc.scalar.copy)
+        def scatter(window, slots, sums, staged):
+            nc.scalar.copy(staged, sums)
+            nc.vector.tensor_copy(window[:].indirect(offsets[:, slots.start // 16 : slots.stop // 16]), staged)
+
+        form_h(0, banks[6])
+        xm_low = prepare_xm(0, "ts_cols")
+        product(banks[3][:], xm_low, slice(0, P), E4M3, hr_mx, slice(0, N), E5M2)
+        form_h(1, banks[0])
+        dw0 = sb.tile([P, N], F32, name="dw0")
+        scatter(windows[0], slice(0, HALF), banks[3][:, HALF:N], dw0[:, 0:HALF])
         quantise_w_i(0, w_i0)
-        xm_high = prepare_xm(1, "coef", nc.vector.tensor_copy)
 
-        dw_banks = [banks[3], banks[4], banks[5], banks[0]]
-
-        def dw_products(half, xm_mx):
-            for k in range(2):
-                product(dw_banks[2 * half + k][:], xm_mx, slice(P * k, P * (k + 1)), E4M3, hr_mx, E5M2)
-
-        def scatter(c, dw):
-            nc.scalar.copy(dw, dw_banks[c][:])
-            nc.vector.tensor_copy(windows[c % 2][:].indirect(offsets[:]), dw)
-            nc.sync.dma_start(out_0[P * c : P * (c + 1), :], windows[c % 2][:])
-
-        dw_products(0, xm_low)
-        dw_products(1, xm_high)
+        dw_banks = [banks[4], banks[5], banks[6], banks[7]]
+        all_slots = slice(HALF, HALF + N)
         for c in range(2):
-            dw = sb.tile([P, N], F32, name="dw%d" % c)
-            scatter(c, dw[:])
+            product(dw_banks[c][:], xm_low, slice(P * c, P * (c + 1)), E4M3, hr_mx, all_slots, E5M2)
+        scatter(windows[0], slice(HALF, N), dw_banks[0][:, HALF:N], dw0[:, HALF:N])
+        nc.sync.dma_start(out_0[0:P, :], windows[0][:])
+        dw1 = sb.tile([P, N], F32, name="dw1")
+        scatter(windows[1], slice(0, N), dw_banks[1][:], dw1[:])
+        nc.sync.dma_start(out_0[P : 2 * P, :], windows[1][:])
+        xm_high = prepare_xm(1, "h_all")
+        for c in range(2):
+            product(dw_banks[2 + c][:], xm_high, slice(P * c, P * (c + 1)), E4M3, hr_mx, all_slots, E5M2)
 
         quantise_w_i(1, turn_w(1, banks[2], "xm0_codes"))
         hi_mx = mx_tiles("hi", R)
@@ -221,11 +230,12 @@ def tile_attend_gnce_wx_ts_kernel(tc, xT, wT, y, wt, ts, xm, offs, out_0, out_1)
             )
         quantise(hi_mx, slice(0, R), h_i[:].rearrange("s p u x -> s (p u x)"), E5M2)
         dw23 = sb.tile([P, 2 * N], F32, name="dw23", tag="h_r", align_bytes=64)
-        scatter(2, dw23[:, 0:N])
-        scatter(3, dw23[:, N : 2 * N])
-        gx_banks = [banks[6], banks[7], banks[1], banks[2]]
+        for c in range(2):
+            scatter(windows[c], slice(0, N), dw_banks[2 + c][:], dw23[:, N * c : N * (c + 1)])
+            nc.sync.dma_start(out_0[P * (2 + c) : P * (3 + c), :], windows[c][:])
+        gx_banks = [banks[0], banks[3], banks[1], banks[2]]
         for c in range(R // P):
-            product(gx_banks[c][:], hi_mx, slice(P * c, P * (c + 1)), E5M2, wi_mx, E4M3)
+            product(gx_banks[c][:], hi_mx, slice(P * c, P * (c + 1)), E5M2, wi_mx, slice(0, D), E4M3)
             gx = sb.tile([P, P, 2, 2], F32, name="gx%d" % c)
             nc.scalar.copy(gx[:], gx_banks[c][:].rearrange("r (u p e) -> r p u e", u=2, e=2))
             nc.scalar.dma_start(out_1[0, P * c : P * (c + 1), :], gx[:].rearrange("r p u e -> r (p u e)"))

from contextlib import ExitStack

import concourse.mybir as mybir
from concourse.masks import make_identity

N, T, D, R = 512, 2048, 512, 512
FLOPS = 3 * 2 * N * D * R

F32 = mybir.dt.float32
BF16 = mybir.dt.bfloat16
I32 = mybir.dt.int32
U32 = mybir.dt.uint32
U16 = mybir.dt.uint16
U8 = mybir.dt.uint8
E4M3 = mybir.dt.float8_e4m3fn_x4
E5M2 = mybir.dt.float8_e5m2_x4
ALU = mybir.AluOpType
ACT = mybir.ActivationFunctionType

P = 128
PACK = 4
HALF = R // 2


def tile_attend_gnce_wx_ts_kernel(tc, xT, wT, y, wt, ts, xm, offs, out_0, out_1):
    nc = tc.nc
    with ExitStack() as ctx:
        sb = ctx.enter_context(tc.tile_pool(name="sb", bufs=1))
        ps = ctx.enter_context(tc.psum_pool(name="ps", bufs=1))

        def mx_tiles(name, width):
            codes = sb.tile([P, width], U32, name=name + "_codes", tag=name + "_codes", align_bytes=64)
            scales = sb.tile([P, width], U8, name=name + "_scales", tag=name + "_scales", align_bytes=64)
            return codes, scales

        def quantise(operand, cols, values, fmt):
            codes, scales = operand
            nc.vector.quantize_mx(out=codes[:, cols].bitcast(fmt), scales=scales[:, cols], in_=values)

        def product(out, stationary, s_cols, s_fmt, moving, m_cols, m_fmt):
            nc.tensor.matmul_mx(
                out=out,
                lhsT=stationary[0][:, s_cols].bitcast(s_fmt),
                lhsT_scale=stationary[1][:, s_cols],
                rhs=moving[0][:, m_cols].bitcast(m_fmt),
                rhs_scale=moving[1][:, m_cols],
                start=True,
                stop=True,
            )

        banks = [ps.tile([P, 512], F32, name="bank%d" % b) for b in range(8)]

        ts_row = sb.tile([1, T], F32, name="ts_row")
        nc.sync.dma_start(ts_row[:], ts[0:1, :])
        offsets = sb.tile([P, N // 16], U16, name="offsets")
        nc.sync.dma_start(offsets[:], offs)
        planes = []
        w_rows = wT.rearrange("(p j) c -> p j c", j=PACK)
        for j in range(PACK):
            plane = sb.tile([P, T], F32, name="w_plane%d" % j)
            nc.sync.dma_start(plane[:], w_rows[:, j, :])
            planes.append(plane)
            if j == 0:
                wt_cols = sb.tile([P, PACK], F32, name="wt_cols")
                nc.sync.dma_start(wt_cols[:], wt[0].rearrange("(p c) o -> p (c o)", c=PACK))
        y_half, x_half = [], []
        x_rows = xT[0].rearrange("(p j) r -> p j r", j=PACK)
        y_rows = y[0].rearrange("(c p) i -> p c i", p=P)
        for h in range(2):
            xt = sb.tile([P, PACK, HALF], F32, name="x_half%d" % h, tag="x_half%d" % h, align_bytes=64)
            nc.sync.dma_start(xt[:], x_rows[:, :, HALF * h : HALF * (h + 1)])
            x_half.append(xt)
            yt = sb.tile([P, 2, N], F32, name="y_half%d" % h)
            nc.sync.dma_start(yt[:], y_rows[:, 2 * h : 2 * h + 2, :])
            y_half.append(yt)
        xm_raw = sb.tile([P, PACK, D], F32, name="xm_raw")
        nc.sync.dma_start(xm_raw[:], xm[0].rearrange("(p j) d -> p j d", j=PACK))

        ts_window = sb.tile([P, T], F32, name="ts_window")
        nc.vector.memset(ts_window[:].bitcast(I32), 0)

        identity = sb.tile([P, P], F32, name="identity")
        make_identity(nc, identity[:])
        warm = sb.tile([P, 1], F32, name="warm")
        nc.scalar.activation(warm[:], identity[:, 0:1], ACT.Sigmoid)

        nc.scalar.copy(ts_window[0:1, :], ts_row[:])
        windows = []
        for c in range(2):
            window = sb.tile([P, T], F32, name="window%d" % c)
            nc.vector.memset(window[:].bitcast(I32), 0)
            windows.append(window)

        hr_mx = mx_tiles("hr", HALF + N)
        nc.vector.memset(hr_mx[0][:, 0:HALF], 0)
        nc.vector.memset(hr_mx[1][:, 0:HALF].bitcast(U32), 0)

        ts_listed = sb.tile([P, N], F32, name="ts_listed")
        nc.vector.tensor_copy(ts_listed[:], ts_window[:].indirect(offsets[:]))
        for t in range(PACK):
            nc.tensor.transpose(banks[7][:, P * t : P * (t + 1)], ts_listed[:, P * t : P * (t + 1)], identity[:])
        ts_cols = sb.tile([P, PACK], F32, name="ts_cols", tag="ts_cols", align_bytes=64)
        nc.scalar.copy(ts_cols[:], banks[7][:, 0:512:P])
        for c in range(PACK):
            nc.tensor.transpose(banks[6][:, P * c : P * (c + 1)], wt_cols[:, c : c + 1].to_broadcast([P, P]), identity[:])
        coef = sb.tile([P, 2, PACK, HALF], F32, name="coef", tag="coef", align_bytes=64)
        for t in range(PACK):
            nc.scalar.activation(
                coef[:, :, t, :].rearrange("p h (n c) -> p h n c", c=PACK),
                banks[6][:].rearrange("p (c h n) -> p h n c", c=PACK, h=2),
                ACT.Copy,
                scale=ts_cols[:, t : t + 1],
            )

        w_d = sb.tile([P, N, PACK], BF16, name="w_d", align_bytes=64)
        w_words = w_d[:].rearrange("p i j -> p (i j)").bitcast(F32)
        wi_mx = mx_tiles("wi", D)
        wd_mx = mx_tiles("wd", N)

        def turn_w(u, bank, tag):
            for t in range(PACK):
                nc.tensor.transpose(bank[:, P * t : P * (t + 1)], w_words[:, 2 * t + u : 2 * N : 2 * PACK], identity[:])
            w_i = sb.tile([P, P, 2, PACK], BF16, name="w_i%d" % u, tag=tag, align_bytes=64)
            nc.scalar.copy(w_i[:], bank[:].bitcast(BF16).rearrange("s (t p e) -> s p e t", t=PACK, e=2))
            return w_i

        def quantise_w_i(u, w_i):
            quantise(wi_mx, slice(HALF * u, HALF * (u + 1)), w_i[:].rearrange("s p e t -> s (p e t)"), E4M3)

        for j in range(PACK):
            nc.vector.tensor_copy(w_d[:, :, j], planes[j][:].indirect(offsets[:]))
        quantise(wd_mx, slice(0, N), w_d[:].rearrange("p i j -> p (i j)"), E4M3)

        h_all = sb.tile([P, PACK * R], BF16, name="h_all", tag="h_all", align_bytes=64)
        h_tiles = h_all[:].rearrange("s (t r) -> s t r", t=PACK)
        x_mxs = []
        for h in range(2):
            x_d = sb.tile([P, HALF, PACK], BF16, name="x_d%d" % h, tag="x_d", align_bytes=64)
            interleave = nc.scalar.copy if h == 0 else nc.vector.tensor_copy
            interleave(x_d[:], x_half[h][:].rearrange("p j r -> p r j"))
            x_mxs.append(mx_tiles("x%d" % h, HALF))
            quantise(x_mxs[h], slice(0, HALF), x_d[:].rearrange("p r j -> p (r j)"), E4M3)
        w_i0 = turn_w(0, banks[1], "x_half0")
        score_banks = [[banks[4], banks[5]], [banks[2], banks[3]]]
        y_banks = [[banks[0], banks[1]], [banks[4], banks[5]]]
        sig = {}
        for h in range(2):
            for q in range(2):
                sig[h, q] = sb.tile([P, 2, HALF], F32, name="sig%d%d" % (h, q))
                for k in range(2):
                    t = 2 * q + k
                    product(score_banks[h][q][:, HALF * k : HALF * (k + 1)], wd_mx, slice(P * t, P * (t + 1)), E4M3, x_mxs[h], slice(0, HALF), E4M3)
                for k in range(2):
                    t = 2 * q + k
                    nc.scalar.activation(
                        sig[h, q][:, k, :], score_banks[h][q][:, HALF * k : HALF * (k + 1)], ACT.Sigmoid, scale=ts_cols[:, t : t + 1]
                    )
                for k in range(2):
                    for c in range(2):
                        nc.tensor.transpose(
                            y_banks[h][q][:, HALF * k + P * c : HALF * k + P * (c + 1)],
                            y_half[h][:, c, P * (2 * q + k) : P * (2 * q + k + 1)],
                            identity[:],
                        )

        h_r = sb.tile([P, 2 * N], F32, name="h_r", tag="h_r", align_bytes=64)

        def form_h(q, bank):
            diff = []
            for h in range(2):
                df = sb.tile([P, 2 * HALF], F32, name="diff%d%d" % (h, q))
                nc.vector.tensor_tensor(df[:], sig[h, q][:].rearrange("p k r -> p (k r)"), y_banks[h][q][:], ALU.subtract)
                diff.append(df)
            for h in range(2):
                nc.vector.tensor_tensor(
                    h_tiles[:, 2 * q : 2 * q + 2, HALF * h : HALF * (h + 1)],
                    diff[h][:].rearrange("p (k r) -> p k r", k=2),
                    coef[:, h, 2 * q : 2 * q + 2, :],
                    ALU.mult,
                )
            words = h_all[:, 2 * R * q : 2 * R * (q + 1)].bitcast(F32)
            for k in range(2):
                for u in range(2):
                    nc.tensor.transpose(bank[:, P * (2 * k + u) : P * (2 * k + u + 1)], words[:, HALF * k + u : HALF * (k + 1) : 2], identity[:])
            part = h_r[:, N * q : N * (q + 1)]
            nc.scalar.copy(part.rearrange("p (k s u) -> p k s u", k=2, u=2), bank[:].rearrange("p (k u s) -> p k s u", k=2, u=2))
            quantise(hr_mx, slice(HALF * (q + 1), HALF * (q + 2)), part.bitcast(BF16), E5M2)

        def prepare_xm(half, tag):
            xm_r = sb.tile([P, HALF, PACK], BF16, name="xm_r%d" % half, tag=tag, align_bytes=64)
            nc.scalar.copy(xm_r[:], xm_raw[:, :, HALF * half : HALF * (half + 1)].rearrange("p j d -> p d j"))
            xm_mx = mx_tiles("xm%d" % half, HALF)
            quantise(xm_mx, slice(0, HALF), xm_r[:].rearrange("p d j -> p (d j)"), E4M3)
            return xm_mx

        def scatter(window, slots, sums, staged):
            nc.scalar.copy(staged, sums)
            nc.vector.tensor_copy(window[:].indirect(offsets[:, slots.start // 16 : slots.stop // 16]), staged)

        form_h(0, banks[6])
        xm_low = prepare_xm(0, "ts_cols")
        product(banks[3][:], xm_low, slice(0, P), E4M3, hr_mx, slice(0, N), E5M2)
        form_h(1, banks[0])
        dw0 = sb.tile([P, N], F32, name="dw0")
        scatter(windows[0], slice(0, HALF), banks[3][:, HALF:N], dw0[:, 0:HALF])
        quantise_w_i(0, w_i0)

        dw_banks = [banks[4], banks[5], banks[6], banks[7]]
        all_slots = slice(HALF, HALF + N)
        for c in range(2):
            product(dw_banks[c][:], xm_low, slice(P * c, P * (c + 1)), E4M3, hr_mx, all_slots, E5M2)
        scatter(windows[0], slice(HALF, N), dw_banks[0][:, HALF:N], dw0[:, HALF:N])
        nc.sync.dma_start(out_0[0:P, :], windows[0][:])
        dw1 = sb.tile([P, N], F32, name="dw1")
        scatter(windows[1], slice(0, N), dw_banks[1][:], dw1[:])
        nc.sync.dma_start(out_0[P : 2 * P, :], windows[1][:])
        xm_high = prepare_xm(1, "h_all")
        for c in range(2):
            product(dw_banks[2 + c][:], xm_high, slice(P * c, P * (c + 1)), E4M3, hr_mx, all_slots, E5M2)

        quantise_w_i(1, turn_w(1, banks[2], "xm0_codes"))
        hi_mx = mx_tiles("hi", R)
        h_i = sb.tile([P, P, 2, 2 * PACK], BF16, name="h_i", align_bytes=64)
        for u in range(2):
            for t in range(PACK):
                nc.tensor.transpose(dw_banks[u][:, P * t : P * (t + 1)], h_r[:, 2 * t + u : 2 * N : 2 * PACK], identity[:])
            nc.scalar.copy(
                h_i[:, :, u, :].rearrange("s p (e t) -> s p e t", e=2),
                dw_banks[u][:].bitcast(BF16).rearrange("s (t p e) -> s p e t", t=PACK, e=2),
            )
        quantise(hi_mx, slice(0, R), h_i[:].rearrange("s p u x -> s (p u x)"), E5M2)
        dw23 = sb.tile([P, 2 * N], F32, name="dw23", tag="h_r", align_bytes=64)
        for c in range(2):
            scatter(windows[c], slice(0, N), dw_banks[2 + c][:], dw23[:, N * c : N * (c + 1)])
            nc.sync.dma_start(out_0[P * (2 + c) : P * (3 + c), :], windows[c][:])
        gx_banks = [banks[0], banks[3], banks[1], banks[2]]
        for c in range(R // P):
            product(gx_banks[c][:], hi_mx, slice(P * c, P * (c + 1)), E5M2, wi_mx, slice(0, D), E4M3)
            gx = sb.tile([P, P, 2, 2], F32, name="gx%d" % c)
            nc.scalar.copy(gx[:], gx_banks[c][:].rearrange("r (u p e) -> r p u e", u=2, e=2))
            nc.scalar.dma_start(out_1[0, P * c : P * (c + 1), :], gx[:].rearrange("r p u e -> r (p u e)"))
